import numpy as np
import ml_dtypes


def mxq(x, axis, fmt="e4m3"):
    dtype, down = {"e4m3": (ml_dtypes.float8_e4m3fn, 7), "e5m2": (ml_dtypes.float8_e5m2, 14)}[fmt]
    v = np.moveaxis(np.asarray(x, np.float32).astype(ml_dtypes.bfloat16).astype(np.float64), axis, -1)
    blocks = v.reshape(v.shape[:-1] + (-1, 32))
    amax = np.abs(blocks).max(-1, keepdims=True)
    byte = np.maximum(np.where(amax > 0, np.frexp(amax)[1] - 1 + 127, 0) - down, 1)
    scale = np.exp2(byte - 127.0)
    codes = (blocks / scale).astype(np.float32).astype(dtype).astype(np.float64)
    return np.moveaxis((codes * scale).reshape(v.shape), -1, axis)


WIDE = False


def mx_kscale(k):
    if not WIDE:
        return np.ones(k)
    levels = np.array([10, -10, 5, -5, 0])
    if k % 512:
        return np.exp2(np.random.permutation(np.resize(levels, k // 32))).repeat(32)
    a = np.empty((k // 512, 16))
    for p in range(k // 512):
        a[p, :8] = np.random.permutation(np.resize(levels, 8))
        for g in range(8):
            far = levels[np.abs(levels - a[p, g]) >= 10]
            a[p, g + 8] = far[np.random.randint(len(far))]
    return np.exp2(a.ravel()).repeat(32)


def f64(x):
    return np.asarray(x).astype(np.float64)


def striped(idx):
    return np.tile(np.asarray(idx).reshape(-1, 16).T, (8, 1)).astype(np.uint16)


def unstriped(offs):
    return offs[:16].T.reshape(-1).astype(np.int64)


E2M1 = np.array([0.0, 0.5, 1.0, 1.5, 2.0, 3.0, 4.0, 6.0, -0.0, -0.5, -1.0, -1.5, -2.0, -3.0, -4.0, -6.0])


def pack_weight(w, fmt):
    k, n = w.shape
    w = f64(np.asarray(w, np.float32).astype(ml_dtypes.bfloat16)).reshape(k // 32, 32, n)
    amax = np.abs(w).max(1)
    if fmt == "e4m3":
        byte = np.frexp(amax)[1] - 1 + 127 - 7
    else:
        mant, ex = np.frexp(amax / 6.0)
        byte = np.where(mant > 0.5, ex, ex - 1) + 127
    byte = np.clip(np.where(amax > 0, byte, 1), 1, 254)
    scaled = (w * np.exp2(127.0 - byte)[:, None, :]).reshape(k, n).astype(np.float32)
    by_word = np.ascontiguousarray(scaled.reshape(k // 512, 128, 4, n).transpose(0, 1, 3, 2))
    if fmt == "e4m3":
        words = by_word.astype(ml_dtypes.float8_e4m3fn).view(np.uint8)
    else:
        c = by_word.astype(ml_dtypes.float4_e2m1fn).view(np.uint8) & 0xF
        words = (c[..., 0::2] | (c[..., 1::2] << 4)).reshape(k // 512, 128, 2 * n)
    return np.ascontiguousarray(words), np.ascontiguousarray(byte.astype(np.uint8).reshape(k // 512, 16, n))


def unpack_weight(words, scales, fmt):
    g, _, n = scales.shape
    words = np.ascontiguousarray(words).reshape(g, 128, n, -1)
    if fmt == "e4m3":
        vals = words.view(ml_dtypes.float8_e4m3fn).astype(np.float64)
    else:
        nib = np.empty((g, 128, n, 4), np.uint8)
        nib[..., 0::2] = words & 0xF
        nib[..., 1::2] = words >> 4
        vals = E2M1[nib]
    vals = vals * np.repeat(np.exp2(scales.astype(np.float64) - 127.0), 8, axis=1)[..., None]
    return vals.transpose(0, 1, 3, 2).reshape(g * 512, n)


K, T, J, N = 512, 2048, 512, 512


def setup_inputs():
    n = np.random.standard_normal
    idx = np.random.permutation(T)[:J]
    fk = mx_kscale(K)
    wp = pack_weight(n((K, N)) * 1 / np.sqrt(K) * fk[:, None], "e2m1")
    return {
        "xf": (n((K, T)) / fk[:, None]).astype(np.float32),
        "ta": (np.random.uniform(0.5, 2.0, (K, 1))).astype(np.float32),
        "tb": (np.random.uniform(-1.0, 1.0, (K, 1))).astype(np.float32),
        "td": (np.random.uniform(-0.7, 0.7, (K, 1))).astype(np.float32),
        "w_words": wp[0],
        "w_scales": wp[1],
        "rw": (np.random.uniform(0.5, 2.0, (1, J))).astype(np.float32),
        "offs": striped(idx),
    }


def reference(xf, ta, tb, td, w_words, w_scales, rw, offs):
    idx = unstriped(offs)
    wu = unpack_weight(w_words, w_scales, "e2m1")
    xg = f64(xf)[:, idx]
    x1 = np.pad(xg, ((0, 0), (1, 0)))[:, :J]
    x2 = np.pad(xg, ((0, 0), (2, 0)))[:, :J]
    u = f64(ta) * xg + f64(tb) * x1 + f64(td) * x2
    uq = mxq(u, 0, "e4m3")
    p = wu.T @ uq
    y = np.maximum(p, 0.0) * f64(rw)
    return y

@@ -1,0 +1,149 @@
+from contextlib import ExitStack
+
+import concourse.mybir as mybir
+from concourse.masks import make_identity
+
+K, T, J, N = 512, 2048, 512, 512
+FLOPS = 2 * K * J * N
+
+F32 = mybir.dt.float32
+BF16 = mybir.dt.bfloat16
+I32 = mybir.dt.int32
+U32 = mybir.dt.uint32
+U16 = mybir.dt.uint16
+U8 = mybir.dt.uint8
+FP8X4 = mybir.dt.float8_e4m3fn_x4
+FP4X4 = mybir.dt.float4_e2m1fn_x4
+ALU = mybir.AluOpType
+ACT = mybir.ActivationFunctionType
+
+P = 128
+PACK = 4
+PAD = 8
+HALF = J // 2
+
+
+def tile_moe_expert_with_taps_kernel(tc, xf, ta, tb, td, w_words, w_scales, rw, offs, out):
+    nc = tc.nc
+    with ExitStack() as ctx:
+        keep = ctx.enter_context(tc.tile_pool(name="keep", bufs=1))
+        psum = ctx.enter_context(tc.psum_pool(name="psum", bufs=1))
+
+        x_rows = xf.rearrange("(p t) c -> p t c", t=PACK)
+        x = [keep.tile([P, T], F32, name=f"x{t}") for t in range(PACK)]
+        offsets = keep.tile([P, J // 16], U16, name="offsets")
+        taps = [keep.tile([P, PACK], F32, name=f"tap{i}") for i in range(3)]
+        rw_cols = keep.tile([P, PACK], F32, name="rw_cols")
+        w = keep.tile([P, 2 * N], U8, name="w", align_bytes=64)
+        w_plane = keep.tile([P, N], U8, name="w_plane", align_bytes=64)
+
+        nc.sync.dma_start(out=x[0][:], in_=x_rows[:, 0, :])
+        nc.sync.dma_start(offsets[:], offs)
+        for i, tap in ((2, td), (1, tb), (0, ta)):
+            nc.sync.dma_start(out=taps[i][:], in_=tap.rearrange("(p t) o -> p (t o)", t=PACK))
+        nc.sync.dma_start(out=rw_cols[:], in_=rw.rearrange("o (p c) -> p (o c)", c=PACK))
+        for t in range(1, PACK):
+            nc.sync.dma_start(out=x[t][:], in_=x_rows[:, t, :])
+        nc.vector.memset(w_plane[:].bitcast(I32), 0)
+        for q in range(4):
+            nc.sync.dma_start(
+                out=w_plane[32 * q : 32 * q + 4, :].bitcast(I32),
+                in_=w_scales[0, 4 * q : 4 * q + 4, :].bitcast(I32),
+            )
+        nc.sync.dma_start(out=w[:].bitcast(I32), in_=w_words[0].bitcast(I32))
+
+        g = [keep.tile([P, PAD + J], F32, name=f"g{t}") for t in range(PACK)]
+        for t in range(PACK):
+            nc.vector.memset(g[t][:, 0:PAD], 0.0)
+
+        ident = keep.tile([P, P], F32, name="ident")
+        make_identity(nc, ident[:])
+        rw_ps = psum.tile([P, PACK, P], F32, name="rw_ps")
+        for c in range(PACK):
+            nc.tensor.transpose(rw_ps[:, c, :], rw_cols[:, c : c + 1].to_broadcast([P, P]), ident[:])
+        rw_all = keep.tile([P, J], F32, name="rw_all")
+        nc.scalar.copy(
+            out=rw_all[:].rearrange("p (b c) -> p b c", c=PACK),
+            in_=rw_ps[:].rearrange("p c b -> p b c"),
+        )
+
+        u_pair = [keep.tile([P, 2, HALF], BF16, name=f"u_pair{i}") for i in range(2)]
+        grouped = [keep.tile([P, HALF, PACK], BF16, name=f"grouped{h}", align_bytes=64) for h in range(2)]
+        a = [[keep.tile([P, HALF], F32, name=f"a{t}{h}") for h in range(2)] for t in range(PACK)]
+        b0 = [keep.tile([P, HALF], F32, name=f"b0{t}") for t in range(PACK)]
+        b1 = keep.tile([P, PACK, HALF], F32, name="b1")
+        c1 = keep.tile([P, PACK, HALF], F32, name="c1")
+
+        def back(t, h, d):
+            return g[t][:, PAD - d + h * HALF : PAD - d + (h + 1) * HALF]
+
+        def gather(t, h):
+            nc.vector.tensor_copy(
+                out=back(t, h, 0), in_=x[t][:].indirect(offsets[:, h * HALF // 16 : (h + 1) * HALF // 16])
+            )
+
+        def tap2(t, h):
+            nc.scalar.activation(out=a[t][h][:], in_=back(t, h, 2), func=ACT.Copy, scale=taps[2][:, t : t + 1])
+
+        def tap1(t, h):
+            nc.vector.scalar_tensor_tensor(
+                out=b0[t][:] if h == 0 else b1[:, t, :], in0=back(t, h, 1), scalar=taps[1][:, t : t + 1],
+                in1=a[t][h][:], op0=ALU.mult, op1=ALU.add,
+            )
+
+        def tap0(t, h):
+            if h == 0:
+                nc.vector.scalar_tensor_tensor(
+                    out=u_pair[t // 2][:, t % 2, :], in0=back(t, 0, 0),
+                    scalar=taps[0][:, t : t + 1], in1=b0[t][:], op0=ALU.mult, op1=ALU.add,
+                )
+            else:
+                nc.scalar.activation(out=c1[:, t, :], in_=back(t, 1, 0), func=ACT.Copy, scale=taps[0][:, t : t + 1])
+
+        def weave(i):
+            nc.scalar.copy(
+                out=grouped[0][:, :, 2 * i : 2 * i + 2], in_=u_pair[i][:].rearrange("p t j -> p j t"),
+            )
+
+        for t in range(PACK):
+            for step in (gather, tap2, tap1, tap0):
+                for h in range(2):
+                    step(t, h)
+            if t % 2 == 1:
+                weave(t // 2)
+        nc.vector.tensor_tensor(
+            out=grouped[1][:].rearrange("p (c i) t -> p c t i", i=2),
+            in0=b1[:].rearrange("p t (c i) -> p c t i", i=2),
+            in1=c1[:].rearrange("p t (c i) -> p c t i", i=2),
+            op=ALU.add,
+        )
+
+        codes = [keep.tile([P, HALF], U32, name=f"codes{h}", align_bytes=64) for h in range(2)]
+        planes = [keep.tile([P, HALF], U8, name=f"plane{h}", align_bytes=64) for h in range(2)]
+        for h in range(2):
+            nc.vector.quantize_mx(
+                out=codes[h][:].bitcast(FP8X4), scales=planes[h][:],
+                in_=grouped[h][:].rearrange("p j t -> p (j t)"),
+            )
+        out_rows = out.rearrange("(m p) j -> p m j", p=P)
+        for h in range(2):
+            cols = slice(h * HALF, (h + 1) * HALF)
+            for mm in range(2):
+                acc = psum.tile([P, 2, HALF], F32, name=f"acc{h}{mm}")
+                for i in range(2):
+                    m = 2 * mm + i
+                    nc.tensor.matmul_mx(
+                        out=acc[:, i, :],
+                        lhsT=w[:, 2 * P * m : 2 * P * (m + 1)].bitcast(FP4X4),
+                        lhsT_scale=w_plane[:, P * m : P * (m + 1)],
+                        rhs=codes[h][:].bitcast(FP8X4),
+                        rhs_scale=planes[h][:],
+                        start=True, stop=True,
+                    )
+                y = keep.tile([P, 2, HALF], F32, name=f"y{h}{mm}")
+                nc.vector.scalar_tensor_tensor(
+                    out=y[:], in0=acc[:], scalar=0.0,
+                    in1=rw_all[:, cols].unsqueeze(1).to_broadcast([P, 2, HALF]),
+                    op0=ALU.max, op1=ALU.mult,
+                )
+                nc.sync.dma_start(out=out_rows[:, 2 * mm : 2 * mm + 2, cols], in_=y[:])

@@ -32,18 +32,23 @@ def tile_moe_expert_with_taps_kernel(tc, xf, ta, tb, td, w_words, w_scales, rw, 
         x_rows = xf.rearrange("(p t) c -> p t c", t=PACK)
         x = [keep.tile([P, T], F32, name=f"x{t}") for t in range(PACK)]
         offsets = keep.tile([P, J // 16], U16, name="offsets")
-        taps = [keep.tile([P, PACK], F32, name=f"tap{i}") for i in range(3)]
+        taps = [None] + [keep.tile([P, PACK], F32, name=f"tap{i}") for i in (1, 2)]
+        ta_rows = ta.rearrange("(p t) o -> p (t o)", t=PACK)
+        ta_parts = [keep.tile([P, n], F32, name=f"ta{i}") for i, n in enumerate((1, 1, 2))]
+        ta_col = [ta_parts[0][:, 0:1], ta_parts[1][:, 0:1], ta_parts[2][:, 0:1], ta_parts[2][:, 1:2]]
         rw_cols = keep.tile([P, PACK], F32, name="rw_cols")
         w = keep.tile([P, 2 * N], U8, name="w", align_bytes=64)
         w_plane = keep.tile([P, N], U8, name="w_plane", align_bytes=64)
 
         nc.sync.dma_start(out=x[0][:], in_=x_rows[:, 0, :])
         nc.sync.dma_start(offsets[:], offs)
-        for i, tap in ((2, td), (1, tb), (0, ta)):
+        for i, tap in ((2, td), (1, tb)):
             nc.sync.dma_start(out=taps[i][:], in_=tap.rearrange("(p t) o -> p (t o)", t=PACK))
         nc.sync.dma_start(out=rw_cols[:], in_=rw.rearrange("o (p c) -> p (o c)", c=PACK))
         for t in range(1, PACK):
             nc.sync.dma_start(out=x[t][:], in_=x_rows[:, t, :])
+            with nc.allow_non_contiguous_dma(reason="one tap a partition"):
+                nc.sync.dma_start(out=ta_parts[t - 1][:], in_=ta_rows[:, t - 1 : (t if t < 3 else 4)])
         nc.vector.memset(w_plane[:].bitcast(I32), 0)
         for q in range(4):
             nc.sync.dma_start(
@@ -52,6 +57,9 @@ def tile_moe_expert_with_taps_kernel(tc, xf, ta, tb, td, w_words, w_scales, rw, 
             )
         nc.sync.dma_start(out=w[:].bitcast(I32), in_=w_words[0].bitcast(I32))
 
+        warm = keep.tile([P, 8], F32, name="warm")
+        nc.vector.memset(warm[:, 0:4], 0.0)
+        nc.scalar.activation(out=warm[:, 4:5], in_=warm[:, 0:1], func=ACT.Copy, scale=warm[:, 1:2])
         g = [keep.tile([P, PAD + J], F32, name=f"g{t}") for t in range(PACK)]
         for t in range(PACK):
             nc.vector.memset(g[t][:, 0:PAD], 0.0)
@@ -68,7 +76,6 @@ def tile_moe_expert_with_taps_kernel(tc, xf, ta, tb, td, w_words, w_scales, rw, 
         )
 
         u_pair = [keep.tile([P, 2, HALF], BF16, name=f"u_pair{i}") for i in range(2)]
-        grouped = [keep.tile([P, HALF, PACK], BF16, name=f"grouped{h}", align_bytes=64) for h in range(2)]
         a = [[keep.tile([P, HALF], F32, name=f"a{t}{h}") for h in range(2)] for t in range(PACK)]
         b0 = [keep.tile([P, HALF], F32, name=f"b0{t}") for t in range(PACK)]
         b1 = keep.tile([P, PACK, HALF], F32, name="b1")
@@ -95,55 +102,86 @@ def tile_moe_expert_with_taps_kernel(tc, xf, ta, tb, td, w_words, w_scales, rw, 
             if h == 0:
                 nc.vector.scalar_tensor_tensor(
                     out=u_pair[t // 2][:, t % 2, :], in0=back(t, 0, 0),
-                    scalar=taps[0][:, t : t + 1], in1=b0[t][:], op0=ALU.mult, op1=ALU.add,
+                    scalar=ta_col[t], in1=b0[t][:], op0=ALU.mult, op1=ALU.add,
                 )
             else:
-                nc.scalar.activation(out=c1[:, t, :], in_=back(t, 1, 0), func=ACT.Copy, scale=taps[0][:, t : t + 1])
+                nc.scalar.activation(out=c1[:, t, :], in_=back(t, 1, 0), func=ACT.Copy, scale=ta_col[t])
 
-        def weave(i):
+        Q = HALF // 2
+        parts = [(0, Q), (Q, Q), (HALF, HALF)]
+        grp = [keep.tile([P, n, PACK], BF16, name=f"grp{q}", align_bytes=64) for q, (j0, n) in enumerate(parts)]
+        codes = [keep.tile([P, n], U32, name=f"codes{q}", align_bytes=64) for q, (j0, n) in enumerate(parts)]
+        planes = [keep.tile([P, n], U8, name=f"plane{q}", align_bytes=64) for q, (j0, n) in enumerate(parts)]
+        banks = [(0, 0, 4), (1, 0, 4), (2, 0, 2), (2, 2, 1), (2, 3, 1)]
+        acc = [psum.tile([P, c, parts[q][1]], F32, name=f"acc{i}") for i, (q, m0, c) in enumerate(banks)]
+        out_rows = out.rearrange("(m p) j -> p m j", p=P)
+
+        def weave(i, q):
             nc.scalar.copy(
-                out=grouped[0][:, :, 2 * i : 2 * i + 2], in_=u_pair[i][:].rearrange("p t j -> p j t"),
+                out=grp[q][:, :, 2 * i : 2 * i + 2],
+                in_=u_pair[i][:, :, q * Q : (q + 1) * Q].rearrange("p t j -> p j t"),
             )
+
+        def add4(r):
+            cols = slice(r * Q, (r + 1) * Q)
+            nc.vector.tensor_tensor(
+                out=grp[2][:, cols, :].rearrange("p (c i) t -> p c t i", i=2),
+                in0=b1[:, :, cols].rearrange("p t (c i) -> p c t i", i=2),
+                in1=c1[:, :, cols].rearrange("p t (c i) -> p c t i", i=2),
+                op=ALU.add,
+            )
+
+        def quant(q):
+            nc.vector.quantize_mx(
+                out=codes[q][:].bitcast(FP8X4), scales=planes[q][:],
+                in_=grp[q][:].rearrange("p j t -> p (j t)"),
+            )
+            for i, (qq, m0, c) in enumerate(banks):
+                if qq == q:
+                    for m in range(m0, m0 + c):
+                        nc.tensor.matmul_mx(
+                            out=acc[i][:, m - m0, :],
+                            lhsT=w[:, 2 * P * m : 2 * P * (m + 1)].bitcast(FP4X4),
+                            lhsT_scale=w_plane[:, P * m : P * (m + 1)],
+                            rhs=codes[q][:].bitcast(FP8X4),
+                            rhs_scale=planes[q][:],
+                            start=True, stop=True,
+                        )
+
+        def finish(i):
+            q, m0, c = banks[i]
+            j0, n = parts[q]
+            y = keep.tile([P, c, n], F32, name=f"y{i}")
+            nc.vector.scalar_tensor_tensor(
+                out=y[:], in0=acc[i][:], scalar=0.0,
+                in1=rw_all[:, j0 : j0 + n].unsqueeze(1).to_broadcast([P, c, n]),
+                op0=ALU.max, op1=ALU.mult,
+            )
+            nc.sync.dma_start(out=out_rows[:, m0 : m0 + c, j0 : j0 + n], in_=y[:])
 
         for t in range(PACK):
-            for step in (gather, tap2, tap1, tap0):
-                for h in range(2):
-                    step(t, h)
-            if t % 2 == 1:
-                weave(t // 2)
-        nc.vector.tensor_tensor(
-            out=grouped[1][:].rearrange("p (c i) t -> p c t i", i=2),
-            in0=b1[:].rearrange("p t (c i) -> p c t i", i=2),
-            in1=c1[:].rearrange("p t (c i) -> p c t i", i=2),
-            op=ALU.add,
-        )
-
-        codes = [keep.tile([P, HALF], U32, name=f"codes{h}", align_bytes=64) for h in range(2)]
-        planes = [keep.tile([P, HALF], U8, name=f"plane{h}", align_bytes=64) for h in range(2)]
-        for h in range(2):
-            nc.vector.quantize_mx(
-                out=codes[h][:].bitcast(FP8X4), scales=planes[h][:],
-                in_=grouped[h][:].rearrange("p j t -> p (j t)"),
-            )
-        out_rows = out.rearrange("(m p) j -> p m j", p=P)
-        for h in range(2):
-            cols = slice(h * HALF, (h + 1) * HALF)
-            for mm in range(2):
-                acc = psum.tile([P, 2, HALF], F32, name=f"acc{h}{mm}")
-                for i in range(2):
-                    m = 2 * mm + i
-                    nc.tensor.matmul_mx(
-                        out=acc[:, i, :],
-                        lhsT=w[:, 2 * P * m : 2 * P * (m + 1)].bitcast(FP4X4),
-                        lhsT_scale=w_plane[:, P * m : P * (m + 1)],
-                        rhs=codes[h][:].bitcast(FP8X4),
-                        rhs_scale=planes[h][:],
-                        start=True, stop=True,
-                    )
-                y = keep.tile([P, 2, HALF], F32, name=f"y{h}{mm}")
-                nc.vector.scalar_tensor_tensor(
-                    out=y[:], in0=acc[:], scalar=0.0,
-                    in1=rw_all[:, cols].unsqueeze(1).to_broadcast([P, 2, HALF]),
-                    op0=ALU.max, op1=ALU.mult,
-                )
-                nc.sync.dma_start(out=out_rows[:, 2 * mm : 2 * mm + 2, cols], in_=y[:])
+            gather(t, 0)
+            gather(t, 1)
+            tap2(t, 0)
+            tap2(t, 1)
+            if t > 0:
+                tap0(t - 1, 0)
+                tap0(t - 1, 1)
+            if t == 2:
+                weave(0, 0)
+                weave(0, 1)
+            tap1(t, 0)
+            if t < PACK - 1:
+                tap1(t, 1)
+        tap0(3, 0)
+        tap1(3, 1)
+        tap0(3, 1)
+        weave(1, 0)
+        weave(1, 1)
+        add4(0)
+        quant(0)
+        quant(1)
+        add4(1)
+        quant(2)
+        for i in range(len(banks)):
+            finish(i)

@@ -75,60 +75,47 @@ def tile_moe_expert_with_taps_kernel(tc, xf, ta, tb, td, w_words, w_scales, rw, 
             in_=rw_ps[:].rearrange("p c b -> p b c"),
         )
 
-        u_pair = [keep.tile([P, 2, HALF], BF16, name=f"u_pair{i}") for i in range(2)]
+        Q = HALF // 2
+        u = keep.tile([P, PACK, J], BF16, name="u")
         a = [[keep.tile([P, HALF], F32, name=f"a{t}{h}") for h in range(2)] for t in range(PACK)]
-        b0 = [keep.tile([P, HALF], F32, name=f"b0{t}") for t in range(PACK)]
-        b1 = keep.tile([P, PACK, HALF], F32, name="b1")
-        c1 = keep.tile([P, PACK, HALF], F32, name="c1")
+        b = [keep.tile([P, J], F32, name=f"b{t}") for t in range(PACK)]
+        grp = [keep.tile([P, Q, PACK], BF16, name=f"grp{q}", align_bytes=64) for q in range(4)]
+        codes = [keep.tile([P, Q], U32, name=f"codes{q}", align_bytes=64) for q in range(4)]
+        planes = [keep.tile([P, Q], U8, name=f"plane{q}", align_bytes=64) for q in range(4)]
+        banks = [(0, 0, 2), (0, 2, 2), (1, 0, 4), (2, 0, 4), (3, 0, 2), (3, 2, 2)]
+        acc = [psum.tile([P, c, Q], F32, name=f"acc{i}") for i, (q, m0, c) in enumerate(banks)]
+        out_rows = out.rearrange("(m p) j -> p m j", p=P)
 
-        def back(t, h, d):
-            return g[t][:, PAD - d + h * HALF : PAD - d + (h + 1) * HALF]
+        def back(t, j0, j1, d):
+            return g[t][:, PAD - d + j0 : PAD - d + j1]
 
         def gather(t, h):
             nc.vector.tensor_copy(
-                out=back(t, h, 0), in_=x[t][:].indirect(offsets[:, h * HALF // 16 : (h + 1) * HALF // 16])
+                out=back(t, h * HALF, (h + 1) * HALF, 0),
+                in_=x[t][:].indirect(offsets[:, h * HALF // 16 : (h + 1) * HALF // 16]),
             )
 
         def tap2(t, h):
-            nc.scalar.activation(out=a[t][h][:], in_=back(t, h, 2), func=ACT.Copy, scale=taps[2][:, t : t + 1])
+            nc.scalar.activation(
+                out=a[t][h][:], in_=back(t, h * HALF, (h + 1) * HALF, 2), func=ACT.Copy, scale=taps[2][:, t : t + 1]
+            )
 
         def tap1(t, h):
             nc.vector.scalar_tensor_tensor(
-                out=b0[t][:] if h == 0 else b1[:, t, :], in0=back(t, h, 1), scalar=taps[1][:, t : t + 1],
-                in1=a[t][h][:], op0=ALU.mult, op1=ALU.add,
+                out=b[t][:, h * HALF : (h + 1) * HALF], in0=back(t, h * HALF, (h + 1) * HALF, 1),
+                scalar=taps[1][:, t : t + 1], in1=a[t][h][:], op0=ALU.mult, op1=ALU.add,
             )
 
-        def tap0(t, h):
-            if h == 0:
-                nc.vector.scalar_tensor_tensor(
-                    out=u_pair[t // 2][:, t % 2, :], in0=back(t, 0, 0),
-                    scalar=ta_col[t], in1=b0[t][:], op0=ALU.mult, op1=ALU.add,
-                )
-            else:
-                nc.scalar.activation(out=c1[:, t, :], in_=back(t, 1, 0), func=ACT.Copy, scale=ta_col[t])
-
-        Q = HALF // 2
-        parts = [(0, Q), (Q, Q), (HALF, HALF)]
-        grp = [keep.tile([P, n, PACK], BF16, name=f"grp{q}", align_bytes=64) for q, (j0, n) in enumerate(parts)]
-        codes = [keep.tile([P, n], U32, name=f"codes{q}", align_bytes=64) for q, (j0, n) in enumerate(parts)]
-        planes = [keep.tile([P, n], U8, name=f"plane{q}", align_bytes=64) for q, (j0, n) in enumerate(parts)]
-        banks = [(0, 0, 4), (1, 0, 4), (2, 0, 2), (2, 2, 1), (2, 3, 1)]
-        acc = [psum.tile([P, c, parts[q][1]], F32, name=f"acc{i}") for i, (q, m0, c) in enumerate(banks)]
-        out_rows = out.rearrange("(m p) j -> p m j", p=P)
-
-        def weave(i, q):
-            nc.scalar.copy(
-                out=grp[q][:, :, 2 * i : 2 * i + 2],
-                in_=u_pair[i][:, :, q * Q : (q + 1) * Q].rearrange("p t j -> p j t"),
+        def tap0(t, j0, j1):
+            nc.vector.scalar_tensor_tensor(
+                out=u[:, t, j0:j1], in0=back(t, j0, j1, 0), scalar=ta_col[t], in1=b[t][:, j0:j1],
+                op0=ALU.mult, op1=ALU.add,
             )
 
-        def add4(r):
-            cols = slice(r * Q, (r + 1) * Q)
-            nc.vector.tensor_tensor(
-                out=grp[2][:, cols, :].rearrange("p (c i) t -> p c t i", i=2),
-                in0=b1[:, :, cols].rearrange("p t (c i) -> p c t i", i=2),
-                in1=c1[:, :, cols].rearrange("p t (c i) -> p c t i", i=2),
-                op=ALU.add,
+        def weave(q, copy):
+            copy(
+                out=grp[q][:].rearrange("p (c i) t -> p c t i", i=4),
+                in_=u[:, :, q * Q : (q + 1) * Q].rearrange("p t (c i) -> p c t i", i=4),
             )
 
         def quant(q):
@@ -150,38 +137,43 @@ def tile_moe_expert_with_taps_kernel(tc, xf, ta, tb, td, w_words, w_scales, rw, 
 
         def finish(i):
             q, m0, c = banks[i]
-            j0, n = parts[q]
-            y = keep.tile([P, c, n], F32, name=f"y{i}")
+            cols = slice(q * Q, (q + 1) * Q)
+            y = keep.tile([P, c, Q], F32, name=f"y{i}")
             nc.vector.scalar_tensor_tensor(
                 out=y[:], in0=acc[i][:], scalar=0.0,
-                in1=rw_all[:, j0 : j0 + n].unsqueeze(1).to_broadcast([P, c, n]),
+                in1=rw_all[:, cols].unsqueeze(1).to_broadcast([P, c, Q]),
                 op0=ALU.max, op1=ALU.mult,
             )
-            nc.sync.dma_start(out=out_rows[:, m0 : m0 + c, j0 : j0 + n], in_=y[:])
+            nc.sync.dma_start(out=out_rows[:, m0 : m0 + c, cols], in_=y[:])
 
-        for t in range(PACK):
+        for t in range(PACK - 1):
             gather(t, 0)
             gather(t, 1)
             tap2(t, 0)
             tap2(t, 1)
             if t > 0:
-                tap0(t - 1, 0)
-                tap0(t - 1, 1)
-            if t == 2:
-                weave(0, 0)
-                weave(0, 1)
+                tap0(t - 1, 0, J)
             tap1(t, 0)
-            if t < PACK - 1:
-                tap1(t, 1)
-        tap0(3, 0)
+            tap1(t, 1)
+        gather(3, 0)
+        gather(3, 1)
+        tap2(3, 0)
+        tap2(3, 1)
+        tap0(2, 0, HALF)
+        tap1(3, 0)
+        tap0(2, HALF, J)
+        tap0(3, 0, HALF)
         tap1(3, 1)
-        tap0(3, 1)
-        weave(1, 0)
-        weave(1, 1)
-        add4(0)
+        weave(0, nc.vector.tensor_copy)
+        weave(1, nc.scalar.copy)
+        tap0(3, HALF, J)
         quant(0)
+        weave(2, nc.scalar.copy)
+        weave(3, nc.scalar.copy)
         quant(1)
-        add4(1)
         quant(2)
-        for i in range(len(banks)):
+        finish(0)
+        finish(1)
+        quant(3)
+        for i in range(2, len(banks)):
             finish(i)

@@ -43,12 +43,12 @@ def tile_moe_expert_with_taps_kernel(tc, xf, ta, tb, td, w_words, w_scales, rw, 
         nc.sync.dma_start(out=x[0][:], in_=x_rows[:, 0, :])
         nc.sync.dma_start(offsets[:], offs)
         for i, tap in ((2, td), (1, tb)):
-            nc.sync.dma_start(out=taps[i][:], in_=tap.rearrange("(p t) o -> p (t o)", t=PACK))
-        nc.sync.dma_start(out=rw_cols[:], in_=rw.rearrange("o (p c) -> p (o c)", c=PACK))
+            nc.scalar.dma_start(out=taps[i][:], in_=tap.rearrange("(p t) o -> p (t o)", t=PACK))
         for t in range(1, PACK):
             nc.sync.dma_start(out=x[t][:], in_=x_rows[:, t, :])
             with nc.allow_non_contiguous_dma(reason="one tap a partition"):
                 nc.sync.dma_start(out=ta_parts[t - 1][:], in_=ta_rows[:, t - 1 : (t if t < 3 else 4)])
+        nc.sync.dma_start(out=rw_cols[:], in_=rw.rearrange("o (p c) -> p (o c)", c=PACK))
         nc.vector.memset(w_plane[:].bitcast(I32), 0)
         for q in range(4):
             nc.sync.dma_start(
@@ -75,15 +75,15 @@ def tile_moe_expert_with_taps_kernel(tc, xf, ta, tb, td, w_words, w_scales, rw, 
             in_=rw_ps[:].rearrange("p c b -> p b c"),
         )
 
-        Q = HALF // 2
+        SC = 96
         u = keep.tile([P, PACK, J], BF16, name="u")
         a = [[keep.tile([P, HALF], F32, name=f"a{t}{h}") for h in range(2)] for t in range(PACK)]
         b = [keep.tile([P, J], F32, name=f"b{t}") for t in range(PACK)]
-        grp = [keep.tile([P, Q, PACK], BF16, name=f"grp{q}", align_bytes=64) for q in range(4)]
-        codes = [keep.tile([P, Q], U32, name=f"codes{q}", align_bytes=64) for q in range(4)]
-        planes = [keep.tile([P, Q], U8, name=f"plane{q}", align_bytes=64) for q in range(4)]
-        banks = [(0, 0, 2), (0, 2, 2), (1, 0, 4), (2, 0, 4), (3, 0, 2), (3, 2, 2)]
-        acc = [psum.tile([P, c, Q], F32, name=f"acc{i}") for i, (q, m0, c) in enumerate(banks)]
+        grp = [keep.tile([P, HALF, PACK], BF16, name=f"grp{q}", align_bytes=64) for q in range(2)]
+        codes = [keep.tile([P, HALF], U32, name=f"codes{q}", align_bytes=64) for q in range(2)]
+        planes = [keep.tile([P, HALF], U8, name=f"plane{q}", align_bytes=64) for q in range(2)]
+        banks = [(0, 0, 1), (0, 1, 1), (0, 2, 2), (1, 0, 2), (1, 2, 1), (1, 3, 1)]
+        acc = [psum.tile([P, c, HALF], F32, name=f"acc{i}") for i, (q, m0, c) in enumerate(banks)]
         out_rows = out.rearrange("(m p) j -> p m j", p=P)
 
         def back(t, j0, j1, d):
@@ -112,10 +112,10 @@ def tile_moe_expert_with_taps_kernel(tc, xf, ta, tb, td, w_words, w_scales, rw, 
                 op0=ALU.mult, op1=ALU.add,
             )
 
-        def weave(q, copy):
+        def weave(h, j0, j1, copy):
             copy(
-                out=grp[q][:].rearrange("p (c i) t -> p c t i", i=4),
-                in_=u[:, :, q * Q : (q + 1) * Q].rearrange("p t (c i) -> p c t i", i=4),
+                out=grp[h][:, j0:j1, :].rearrange("p (c i) t -> p c t i", i=4),
+                in_=u[:, :, h * HALF + j0 : h * HALF + j1].rearrange("p t (c i) -> p c t i", i=4),
             )
 
         def quant(q):
@@ -137,14 +137,15 @@ def tile_moe_expert_with_taps_kernel(tc, xf, ta, tb, td, w_words, w_scales, rw, 
 
         def finish(i):
             q, m0, c = banks[i]
-            cols = slice(q * Q, (q + 1) * Q)
-            y = keep.tile([P, c, Q], F32, name=f"y{i}")
+            cols = slice(q * HALF, (q + 1) * HALF)
+            y = keep.tile([P, c, HALF], F32, name=f"y{i}")
             nc.vector.scalar_tensor_tensor(
                 out=y[:], in0=acc[i][:], scalar=0.0,
-                in1=rw_all[:, cols].unsqueeze(1).to_broadcast([P, c, Q]),
+                in1=rw_all[:, cols].unsqueeze(1).to_broadcast([P, c, HALF]),
                 op0=ALU.max, op1=ALU.mult,
             )
-            nc.sync.dma_start(out=out_rows[:, m0 : m0 + c, cols], in_=y[:])
+            queue = nc.sync if i % 2 == 0 else nc.scalar
+            queue.dma_start(out=out_rows[:, m0 : m0 + c, cols], in_=y[:])
 
         for t in range(PACK - 1):
             gather(t, 0)
@@ -164,16 +165,12 @@ def tile_moe_expert_with_taps_kernel(tc, xf, ta, tb, td, w_words, w_scales, rw, 
         tap0(2, HALF, J)
         tap0(3, 0, HALF)
         tap1(3, 1)
-        weave(0, nc.vector.tensor_copy)
-        weave(1, nc.scalar.copy)
+        weave(0, SC, HALF, nc.vector.tensor_copy)
+        weave(0, 0, SC, nc.scalar.copy)
         tap0(3, HALF, J)
         quant(0)
-        weave(2, nc.scalar.copy)
-        weave(3, nc.scalar.copy)
+        weave(1, 0, SC, nc.scalar.copy)
+        weave(1, SC, HALF, nc.vector.tensor_copy)
         quant(1)
-        quant(2)
-        finish(0)
-        finish(1)
-        quant(3)
-        for i in range(2, len(banks)):
+        for i in range(len(banks)):
             finish(i)

@@ -44,11 +44,11 @@ def tile_moe_expert_with_taps_kernel(tc, xf, ta, tb, td, w_words, w_scales, rw, 
         nc.sync.dma_start(offsets[:], offs)
         for i, tap in ((2, td), (1, tb)):
             nc.scalar.dma_start(out=taps[i][:], in_=tap.rearrange("(p t) o -> p (t o)", t=PACK))
+        nc.scalar.dma_start(out=rw_cols[:], in_=rw.rearrange("o (p c) -> p (o c)", c=PACK))
         for t in range(1, PACK):
             nc.sync.dma_start(out=x[t][:], in_=x_rows[:, t, :])
             with nc.allow_non_contiguous_dma(reason="one tap a partition"):
                 nc.sync.dma_start(out=ta_parts[t - 1][:], in_=ta_rows[:, t - 1 : (t if t < 3 else 4)])
-        nc.sync.dma_start(out=rw_cols[:], in_=rw.rearrange("o (p c) -> p (o c)", c=PACK))
         nc.vector.memset(w_plane[:].bitcast(I32), 0)
         for q in range(4):
             nc.sync.dma_start(
@@ -66,7 +66,7 @@ def tile_moe_expert_with_taps_kernel(tc, xf, ta, tb, td, w_words, w_scales, rw, 
 
         ident = keep.tile([P, P], F32, name="ident")
         make_identity(nc, ident[:])
-        rw_ps = psum.tile([P, PACK, P], F32, name="rw_ps")
+        rw_ps = psum.tile([P, PACK, P], F32, name="rw_ps", tag="acc7")
         for c in range(PACK):
             nc.tensor.transpose(rw_ps[:, c, :], rw_cols[:, c : c + 1].to_broadcast([P, P]), ident[:])
         rw_all = keep.tile([P, J], F32, name="rw_all")
@@ -82,8 +82,8 @@ def tile_moe_expert_with_taps_kernel(tc, xf, ta, tb, td, w_words, w_scales, rw, 
         grp = [keep.tile([P, HALF, PACK], BF16, name=f"grp{q}", align_bytes=64) for q in range(2)]
         codes = [keep.tile([P, HALF], U32, name=f"codes{q}", align_bytes=64) for q in range(2)]
         planes = [keep.tile([P, HALF], U8, name=f"plane{q}", align_bytes=64) for q in range(2)]
-        banks = [(0, 0, 1), (0, 1, 1), (0, 2, 2), (1, 0, 2), (1, 2, 1), (1, 3, 1)]
-        acc = [psum.tile([P, c, HALF], F32, name=f"acc{i}") for i, (q, m0, c) in enumerate(banks)]
+        banks = [(h, m, 1) for h in range(2) for m in range(4)]
+        acc = [psum.tile([P, c, HALF], F32, name=f"acc{i}", tag=f"acc{i}") for i, (q, m0, c) in enumerate(banks)]
         out_rows = out.rearrange("(m p) j -> p m j", p=P)
 
         def back(t, j0, j1, d):

from contextlib import ExitStack

import concourse.mybir as mybir
from concourse.masks import make_identity

K, T, J, N = 512, 2048, 512, 512
FLOPS = 2 * K * J * N

F32 = mybir.dt.float32
BF16 = mybir.dt.bfloat16
I32 = mybir.dt.int32
U32 = mybir.dt.uint32
U16 = mybir.dt.uint16
U8 = mybir.dt.uint8
FP8X4 = mybir.dt.float8_e4m3fn_x4
FP4X4 = mybir.dt.float4_e2m1fn_x4
ALU = mybir.AluOpType
ACT = mybir.ActivationFunctionType

P = 128
PACK = 4
PAD = 8
HALF = J // 2


def tile_moe_expert_with_taps_kernel(tc, xf, ta, tb, td, w_words, w_scales, rw, offs, out):
    nc = tc.nc
    with ExitStack() as ctx:
        keep = ctx.enter_context(tc.tile_pool(name="keep", bufs=1))
        psum = ctx.enter_context(tc.psum_pool(name="psum", bufs=1))

        x_rows = xf.rearrange("(p t) c -> p t c", t=PACK)
        x = [keep.tile([P, T], F32, name=f"x{t}") for t in range(PACK)]
        offsets = keep.tile([P, J // 16], U16, name="offsets")
        taps = [None] + [keep.tile([P, PACK], F32, name=f"tap{i}") for i in (1, 2)]
        ta_rows = ta.rearrange("(p t) o -> p (t o)", t=PACK)
        ta_parts = [keep.tile([P, n], F32, name=f"ta{i}") for i, n in enumerate((1, 1, 2))]
        ta_col = [ta_parts[0][:, 0:1], ta_parts[1][:, 0:1], ta_parts[2][:, 0:1], ta_parts[2][:, 1:2]]
        rw_cols = keep.tile([P, PACK], F32, name="rw_cols")
        w = keep.tile([P, 2 * N], U8, name="w", align_bytes=64)
        w_plane = keep.tile([P, N], U8, name="w_plane", align_bytes=64)

        nc.sync.dma_start(out=x[0][:], in_=x_rows[:, 0, :])
        nc.sync.dma_start(offsets[:], offs)
        for i, tap in ((2, td), (1, tb)):
            nc.scalar.dma_start(out=taps[i][:], in_=tap.rearrange("(p t) o -> p (t o)", t=PACK))
        nc.scalar.dma_start(out=rw_cols[:], in_=rw.rearrange("o (p c) -> p (o c)", c=PACK))
        for t in range(1, PACK):
            nc.sync.dma_start(out=x[t][:], in_=x_rows[:, t, :])
            with nc.allow_non_contiguous_dma(reason="one tap a partition"):
                nc.sync.dma_start(out=ta_parts[t - 1][:], in_=ta_rows[:, t - 1 : (t if t < 3 else 4)])
        nc.vector.memset(w_plane[:].bitcast(I32), 0)
        for q in range(4):
            nc.sync.dma_start(
                out=w_plane[32 * q : 32 * q + 4, :].bitcast(I32),
                in_=w_scales[0, 4 * q : 4 * q + 4, :].bitcast(I32),
            )
        nc.sync.dma_start(out=w[:].bitcast(I32), in_=w_words[0].bitcast(I32))

        warm = keep.tile([P, 8], F32, name="warm")
        nc.vector.memset(warm[:, 0:4], 0.0)
        nc.scalar.activation(out=warm[:, 4:5], in_=warm[:, 0:1], func=ACT.Copy, scale=warm[:, 1:2])
        g = [keep.tile([P, PAD + J], F32, name=f"g{t}") for t in range(PACK)]
        for t in range(PACK):
            nc.vector.memset(g[t][:, 0:PAD], 0.0)

        ident = keep.tile([P, P], F32, name="ident")
        make_identity(nc, ident[:])
        rw_ps = psum.tile([P, PACK, P], F32, name="rw_ps", tag="acc7")
        for c in range(PACK):
            nc.tensor.transpose(rw_ps[:, c, :], rw_cols[:, c : c + 1].to_broadcast([P, P]), ident[:])
        rw_all = keep.tile([P, J], F32, name="rw_all")
        nc.scalar.copy(
            out=rw_all[:].rearrange("p (b c) -> p b c", c=PACK),
            in_=rw_ps[:].rearrange("p c b -> p b c"),
        )

        SC = 96
        u = keep.tile([P, PACK, J], BF16, name="u")
        a = [[keep.tile([P, HALF], F32, name=f"a{t}{h}") for h in range(2)] for t in range(PACK)]
        b = [keep.tile([P, J], F32, name=f"b{t}") for t in range(PACK)]
        grp = [keep.tile([P, HALF, PACK], BF16, name=f"grp{q}", align_bytes=64) for q in range(2)]
        codes = [keep.tile([P, HALF], U32, name=f"codes{q}", align_bytes=64) for q in range(2)]
        planes = [keep.tile([P, HALF], U8, name=f"plane{q}", align_bytes=64) for q in range(2)]
        banks = [(h, m, 1) for h in range(2) for m in range(4)]
        acc = [psum.tile([P, c, HALF], F32, name=f"acc{i}", tag=f"acc{i}") for i, (q, m0, c) in enumerate(banks)]
        out_rows = out.rearrange("(m p) j -> p m j", p=P)

        def back(t, j0, j1, d):
            return g[t][:, PAD - d + j0 : PAD - d + j1]

        def gather(t, h):
            nc.vector.tensor_copy(
                out=back(t, h * HALF, (h + 1) * HALF, 0),
                in_=x[t][:].indirect(offsets[:, h * HALF // 16 : (h + 1) * HALF // 16]),
            )

        def tap2(t, h):
            nc.scalar.activation(
                out=a[t][h][:], in_=back(t, h * HALF, (h + 1) * HALF, 2), func=ACT.Copy, scale=taps[2][:, t : t + 1]
            )

        def tap1(t, h):
            nc.vector.scalar_tensor_tensor(
                out=b[t][:, h * HALF : (h + 1) * HALF], in0=back(t, h * HALF, (h + 1) * HALF, 1),
                scalar=taps[1][:, t : t + 1], in1=a[t][h][:], op0=ALU.mult, op1=ALU.add,
            )

        def tap0(t, j0, j1):
            nc.vector.scalar_tensor_tensor(
                out=u[:, t, j0:j1], in0=back(t, j0, j1, 0), scalar=ta_col[t], in1=b[t][:, j0:j1],
                op0=ALU.mult, op1=ALU.add,
            )

        def weave(h, j0, j1, copy):
            copy(
                out=grp[h][:, j0:j1, :].rearrange("p (c i) t -> p c t i", i=4),
                in_=u[:, :, h * HALF + j0 : h * HALF + j1].rearrange("p t (c i) -> p c t i", i=4),
            )

        def quant(q):
            nc.vector.quantize_mx(
                out=codes[q][:].bitcast(FP8X4), scales=planes[q][:],
                in_=grp[q][:].rearrange("p j t -> p (j t)"),
            )
            for i, (qq, m0, c) in enumerate(banks):
                if qq == q:
                    for m in range(m0, m0 + c):
                        nc.tensor.matmul_mx(
                            out=acc[i][:, m - m0, :],
                            lhsT=w[:, 2 * P * m : 2 * P * (m + 1)].bitcast(FP4X4),
                            lhsT_scale=w_plane[:, P * m : P * (m + 1)],
                            rhs=codes[q][:].bitcast(FP8X4),
                            rhs_scale=planes[q][:],
                            start=True, stop=True,
                        )

        def finish(i):
            q, m0, c = banks[i]
            cols = slice(q * HALF, (q + 1) * HALF)
            y = keep.tile([P, c, HALF], F32, name=f"y{i}")
            nc.vector.scalar_tensor_tensor(
                out=y[:], in0=acc[i][:], scalar=0.0,
                in1=rw_all[:, cols].unsqueeze(1).to_broadcast([P, c, HALF]),
                op0=ALU.max, op1=ALU.mult,
            )
            queue = nc.sync if i % 2 == 0 else nc.scalar
            queue.dma_start(out=out_rows[:, m0 : m0 + c, cols], in_=y[:])

        for t in range(PACK - 1):
            gather(t, 0)
            gather(t, 1)
            tap2(t, 0)
            tap2(t, 1)
            if t > 0:
                tap0(t - 1, 0, J)
            tap1(t, 0)
            tap1(t, 1)
        gather(3, 0)
        gather(3, 1)
        tap2(3, 0)
        tap2(3, 1)
        tap0(2, 0, HALF)
        tap1(3, 0)
        tap0(2, HALF, J)
        tap0(3, 0, HALF)
        tap1(3, 1)
        weave(0, SC, HALF, nc.vector.tensor_copy)
        weave(0, 0, SC, nc.scalar.copy)
        tap0(3, HALF, J)
        quant(0)
        weave(1, 0, SC, nc.scalar.copy)
        weave(1, SC, HALF, nc.vector.tensor_copy)
        quant(1)
        for i in range(len(banks)):
            finish(i)
